import numpy as np
import ml_dtypes


def mxq(x, axis, fmt="e4m3"):
    dtype, down = {"e4m3": (ml_dtypes.float8_e4m3fn, 7), "e5m2": (ml_dtypes.float8_e5m2, 14)}[fmt]
    v = np.moveaxis(np.asarray(x, np.float32).astype(ml_dtypes.bfloat16).astype(np.float64), axis, -1)
    blocks = v.reshape(v.shape[:-1] + (-1, 32))
    amax = np.abs(blocks).max(-1, keepdims=True)
    byte = np.maximum(np.where(amax > 0, np.frexp(amax)[1] - 1 + 127, 0) - down, 1)
    scale = np.exp2(byte - 127.0)
    codes = (blocks / scale).astype(np.float32).astype(dtype).astype(np.float64)
    return np.moveaxis((codes * scale).reshape(v.shape), -1, axis)


WIDE = False


def mx_kscale(k):
    if not WIDE:
        return np.ones(k)
    levels = np.array([10, -10, 5, -5, 0])
    if k % 512:
        return np.exp2(np.random.permutation(np.resize(levels, k // 32))).repeat(32)
    a = np.empty((k // 512, 16))
    for p in range(k // 512):
        a[p, :8] = np.random.permutation(np.resize(levels, 8))
        for g in range(8):
            far = levels[np.abs(levels - a[p, g]) >= 10]
            a[p, g + 8] = far[np.random.randint(len(far))]
    return np.exp2(a.ravel()).repeat(32)


def f64(x):
    return np.asarray(x).astype(np.float64)


def striped8(idx):
    return np.asarray(idx).reshape(8, -1, 16).transpose(0, 2, 1).reshape(128, -1).astype(np.uint16)


def unstriped8(offs):
    return offs.reshape(8, 16, -1).transpose(0, 2, 1).reshape(8, -1).astype(np.int64)


def pick8(x, idx, run):
    r = np.arange(len(x))
    return x[r[:, None], idx[r % (8 * run) // run]]


E2M1 = np.array([0.0, 0.5, 1.0, 1.5, 2.0, 3.0, 4.0, 6.0, -0.0, -0.5, -1.0, -1.5, -2.0, -3.0, -4.0, -6.0])


def pack_weight(w, fmt):
    k, n = w.shape
    w = f64(np.asarray(w, np.float32).astype(ml_dtypes.bfloat16)).reshape(k // 32, 32, n)
    amax = np.abs(w).max(1)
    if fmt == "e4m3":
        byte = np.frexp(amax)[1] - 1 + 127 - 7
    else:
        mant, ex = np.frexp(amax / 6.0)
        byte = np.where(mant > 0.5, ex, ex - 1) + 127
    byte = np.clip(np.where(amax > 0, byte, 1), 1, 254)
    scaled = (w * np.exp2(127.0 - byte)[:, None, :]).reshape(k, n).astype(np.float32)
    by_word = np.ascontiguousarray(scaled.reshape(k // 512, 128, 4, n).transpose(0, 1, 3, 2))
    if fmt == "e4m3":
        words = by_word.astype(ml_dtypes.float8_e4m3fn).view(np.uint8)
    else:
        c = by_word.astype(ml_dtypes.float4_e2m1fn).view(np.uint8) & 0xF
        words = (c[..., 0::2] | (c[..., 1::2] << 4)).reshape(k // 512, 128, 2 * n)
    return np.ascontiguousarray(words), np.ascontiguousarray(byte.astype(np.uint8).reshape(k // 512, 16, n))


def unpack_weight(words, scales, fmt):
    g, _, n = scales.shape
    words = np.ascontiguousarray(words).reshape(g, 128, n, -1)
    if fmt == "e4m3":
        vals = words.view(ml_dtypes.float8_e4m3fn).astype(np.float64)
    else:
        nib = np.empty((g, 128, n, 4), np.uint8)
        nib[..., 0::2] = words & 0xF
        nib[..., 1::2] = words >> 4
        vals = E2M1[nib]
    vals = vals * np.repeat(np.exp2(scales.astype(np.float64) - 127.0), 8, axis=1)[..., None]
    return vals.transpose(0, 1, 3, 2).reshape(g * 512, n)


D, T, U, X, I, Q, E = 512, 1024, 1024, 1024, 512, 512, 256


def setup_inputs():
    n = np.random.standard_normal
    idx = np.stack([np.random.permutation(T)[:I] for _ in range(8)])
    idx2 = np.stack([np.random.permutation(U)[:I] for _ in range(8)])
    idx3 = np.stack([np.random.permutation(T)[:I] for _ in range(8)])
    idx4 = np.stack([np.random.permutation(X)[:I] for _ in range(8)])
    idx5 = np.stack([np.random.permutation(X)[:I] for _ in range(8)])
    fd = mx_kscale(D)
    fq = mx_kscale(Q)
    keysp = pack_weight(n((D, T)) / fd[:, None], "e4m3")
    notesp = pack_weight(n((D, U)) / fd[:, None], "e2m1")
    usersp = pack_weight(n((D, X)) / fd[:, None], "e2m1")
    mixp = pack_weight(n((Q, E)) * 1.0 / np.sqrt(Q) / fq[:, None], "e2m1")
    return {
        "query": (n((D, Q)) * 1.0 / np.sqrt(D) * fd[:, None]).astype(np.float32),
        "query2": (n((D, Q)) * 1.0 / np.sqrt(D) * fd[:, None]).astype(np.float32),
        "keys_words": keysp[0],
        "keys_scales": keysp[1],
        "notes_words": notesp[0],
        "notes_scales": notesp[1],
        "users_words": usersp[0],
        "users_scales": usersp[1],
        "rowf": (np.random.uniform(0.5, 2.0, (Q, 1)) * fq[:, None]).astype(np.float32),
        "mix_words": mixp[0],
        "mix_scales": mixp[1],
        "offs": striped8(idx),
        "offs2": striped8(idx2),
        "offs3": striped8(idx3),
        "offs4": striped8(idx4),
        "offs5": striped8(idx5),
    }


def reference(query, query2, keys_words, keys_scales, notes_words, notes_scales, users_words, users_scales, rowf, mix_words, mix_scales, offs, offs2, offs3, offs4, offs5):
    idx = unstriped8(offs)
    idx2 = unstriped8(offs2)
    idx3 = unstriped8(offs3)
    idx4 = unstriped8(offs4)
    idx5 = unstriped8(offs5)
    keysu = unpack_weight(keys_words, keys_scales, "e4m3")
    notesu = unpack_weight(notes_words, notes_scales, "e2m1")
    usersu = unpack_weight(users_words, users_scales, "e2m1")
    mixu = unpack_weight(mix_words, mix_scales, "e2m1")
    queryq = mxq(f64(query), 0, "e4m3")
    a = queryq.T @ keysu
    b = queryq.T @ notesu
    query2q = mxq(f64(query2), 0, "e4m3")
    c0 = query2q.T @ usersu
    r = pick8(b, idx2, 64) - pick8(a, idx, 64)
    f1 = np.zeros((Q, T))
    f1[np.arange(Q)[:, None], idx[np.arange(Q) % 512 // 64]] = r
    a2 = a + f1
    f2 = np.zeros((Q, X))
    f2[np.arange(Q)[:, None], idx4[np.arange(Q) % 512 // 64]] = pick8(a2, idx3, 64)
    cc = c0 - f2
    g = pick8(cc, idx5, 64)
    gw = g * f64(rowf)
    gwq = mxq(gw, 0, "e4m3")
    y = mixu.T @ gwq
    return y

@@ -1,0 +1,217 @@
+from contextlib import ExitStack
+
+import concourse.mybir as mybir
+
+D, T, U, X, I, Q, E = 512, 1024, 1024, 1024, 512, 512, 256
+FLOPS = 2 * D * Q * (T + U + X) + 2 * Q * E * I
+
+F32 = mybir.dt.float32
+BF16 = mybir.dt.bfloat16
+I32 = mybir.dt.int32
+U32 = mybir.dt.uint32
+U16 = mybir.dt.uint16
+U8 = mybir.dt.uint8
+FP8X4 = mybir.dt.float8_e4m3fn_x4
+FP4X4 = mybir.dt.float4_e2m1fn_x4
+COPY = mybir.ActivationFunctionType.Copy
+ADD = mybir.AluOpType.add
+SUB = mybir.AluOpType.subtract
+MULT = mybir.AluOpType.mult
+
+P = 128
+PACK = 4
+BANK = 512
+HALF = I // 2
+LIST_COLS = I // 16
+
+
+def tile_attend_correctedthen_threeq_mixed_kernel(
+    tc, query, query2, keys_words, keys_scales, notes_words, notes_scales, users_words, users_scales,
+    rowf, mix_words, mix_scales, offs, offs2, offs3, offs4, offs5, out,
+):
+    nc = tc.nc
+    with ExitStack() as ctx:
+        keep = ctx.enter_context(tc.tile_pool(name="keep", bufs=1))
+        ring = ctx.enter_context(tc.tile_pool(name="ring", bufs=2))
+        score_banks = ctx.enter_context(tc.psum_pool(name="score_banks", bufs=6))
+        user_banks = ctx.enter_context(tc.psum_pool(name="user_banks", bufs=2))
+
+        def load_list(name, src):
+            tile = keep.tile([P, LIST_COLS], U16, name=name)
+            nc.sync.dma_start(tile[:], src)
+            return tile
+
+        def zeroed_plane(engine, name, width):
+            plane = keep.tile([P, width], U8, name=name, align_bytes=64)
+            engine.memset(plane[:].bitcast(I32), 0)
+            return plane
+
+        def load_plane(queue, plane, src):
+            for quad in range(4):
+                queue.dma_start(
+                    plane[32 * quad : 32 * quad + 4, :].bitcast(I32),
+                    src[0, 4 * quad : 4 * quad + 4, :].bitcast(I32),
+                )
+
+        def load_fp4(name, src):
+            words = keep.tile([P, src.shape[2]], U8, name=name, align_bytes=64)
+            nc.sync.dma_start(words[:].bitcast(I32), src[0].bitcast(I32))
+            return words
+
+        def load_rows(src):
+            raw = keep.tile([P, PACK, Q], F32, name="raw")
+            nc.sync.dma_start(raw[:], src.rearrange("(p j) q -> p j q", j=PACK))
+            return raw
+
+        def deal(copy, name, raw, pair):
+            dealt = keep.tile([P, 2 * P * PACK], BF16, name=name, align_bytes=64)
+            copy(
+                dealt[:].rearrange("p (r m j) -> p m r j", r=2, j=PACK),
+                raw[:].rearrange("p j (m r) -> p m r j", r=PACK)[:, :, 2 * pair : 2 * pair + 2, :],
+            )
+            return dealt
+
+        def quantise(name, values):
+            width = values.shape[1] // PACK
+            codes = keep.tile([P, width], U32, name=name + "_codes", align_bytes=64)
+            scales = keep.tile([P, width], U8, name=name + "_scales", align_bytes=64)
+            nc.vector.quantize_mx(out=codes[:].bitcast(FP8X4), scales=scales[:], in_=values)
+            return [(codes[:, c : c + P].bitcast(FP8X4), scales[:, c : c + P]) for c in range(0, width, P)]
+
+        def scores(banks, rows, moving, plane, half):
+            bank = banks.tile([P, BANK], F32, name="bank")
+            nc.tensor.matmul_mx(
+                out=bank[:], lhsT=rows[0], lhsT_scale=rows[1], rhs=moving[half],
+                rhs_scale=plane[:, half * BANK : (half + 1) * BANK], start=True, stop=True,
+            )
+            return bank
+
+        keys_plane = zeroed_plane(nc.vector, "keys_plane", T)
+        notes_plane = zeroed_plane(nc.gpsimd, "notes_plane", U)
+        idx = load_list("idx", offs)
+        idx2 = load_list("idx2", offs2)
+        idx3 = load_list("idx3", offs3)
+        idx4 = load_list("idx4", offs4)
+        idx5 = load_list("idx5", offs5)
+        raw = load_rows(query)
+        load_plane(nc.scalar, keys_plane, keys_scales)
+        load_plane(nc.gpsimd, notes_plane, notes_scales)
+        keys = keep.tile([P, T], U32, name="keys", align_bytes=64)
+        nc.sync.dma_start(keys[:].bitcast(I32), keys_words[0].rearrange("p t j -> p (t j)").bitcast(I32))
+        notes = load_fp4("notes", notes_words)
+
+        users_plane = zeroed_plane(nc.vector, "users_plane", X)
+        mix_plane = zeroed_plane(nc.vector, "mix_plane", E)
+        f1 = [keep.tile([P, T], F32, name="f1_%d" % n) for n in range(2)]
+        f2 = keep.tile([P, X], F32, name="f2")
+        for window in f1 + [f2]:
+            nc.vector.memset(window[:], 0.0)
+
+        keys_moving = [keys[:, h * BANK : (h + 1) * BANK].bitcast(FP8X4) for h in range(2)]
+        notes_moving = [notes[:, 2 * h * BANK : 2 * (h + 1) * BANK].bitcast(FP4X4) for h in range(2)]
+
+        low = deal(nc.vector.tensor_copy, "query_low", raw, 0)
+        high = deal(nc.scalar.copy, "query_high", raw, 1)
+        rows = quantise("rows0", low[:, : P * PACK]) + quantise("rows1", low[:, P * PACK :])
+        rows = rows + quantise("rows23", high[:])
+
+        raw2 = load_rows(query2)
+        users = load_fp4("users", users_words)
+        load_plane(nc.sync, users_plane, users_scales)
+        factors = keep.tile([P, PACK], F32, name="factors")
+        nc.sync.dma_start(factors[:], rowf.rearrange("(p r) o -> p (r o)", r=PACK))
+        mix = load_fp4("mix", mix_words)
+        load_plane(nc.sync, mix_plane, mix_scales)
+        users_moving = [users[:, 2 * h * BANK : 2 * (h + 1) * BANK].bitcast(FP4X4) for h in range(2)]
+
+        rows2 = []
+        a2, cc = {}, {}
+        gw = keep.tile([P, PACK, I], F32, name="gw")
+
+        def first_lookups(r):
+            a = ring.tile([P, T], F32, name="a", bufs=3)
+            b = ring.tile([P, U], F32, name="b")
+            minus_a = ring.tile([P, I], F32, name="minus_a")
+            plus_b = ring.tile([P, I], F32, name="plus_b")
+            helper = nc.vector.tensor_copy if r == 0 else nc.scalar.copy
+            nc.scalar.copy(a[:, :BANK], scores(score_banks, rows[r], keys_moving, keys_plane, 0)[:])
+            helper(a[:, BANK:], scores(score_banks, rows[r], keys_moving, keys_plane, 1)[:])
+            if r == 0:
+                nc.scalar.activation(minus_a[:], a[:].indirect(idx[:]), COPY, scale=-1.0)
+            for half in range(2):
+                helper(b[:, half * BANK : (half + 1) * BANK], scores(score_banks, rows[r], notes_moving, notes_plane, half)[:])
+            if r == 0:
+                nc.vector.tensor_copy(plus_b[:, :HALF], b[:].indirect(idx2[:, : LIST_COLS // 2]))
+                nc.scalar.activation(plus_b[:, HALF:], b[:].indirect(idx2[:, LIST_COLS // 2 :]), COPY)
+            else:
+                nc.scalar.activation(minus_a[:], a[:].indirect(idx[:]), COPY, scale=-1.0)
+                nc.scalar.activation(plus_b[:], b[:].indirect(idx2[:]), COPY)
+            window = f1[r % len(f1)]
+            nc.vector.tensor_tensor(window[:].indirect(idx[:]), plus_b[:], minus_a[:], ADD)
+            a2[r] = keep.tile([P, T], F32, name="a2_%d" % r, tag="a2_%d" % r)
+            adder = nc.vector if r == 0 else nc.gpsimd
+            adder.tensor_tensor(a2[r][:], a[:], window[:], ADD)
+
+        def second_rows(pair):
+            rows2.extend(quantise("rows2_%d" % pair, deal(nc.scalar.copy, "query2_%d" % pair, raw2, pair)[:]))
+
+        def correct_users(r):
+            picked = ring.tile([P, I], F32, name="picked")
+            nc.scalar.activation(picked[:], a2[r][:].indirect(idx3[:]), COPY)
+            nc.vector.tensor_copy(f2[:].indirect(idx4[:]), picked[:])
+            cc[r] = ring.tile([P, X], F32, name="cc")
+            for half in range(2):
+                cols = slice(half * BANK, (half + 1) * BANK)
+                c0 = scores(user_banks, rows2[r], users_moving, users_plane, half)
+                nc.vector.tensor_tensor(cc[r][:, cols], c0[:], f2[:, cols], SUB)
+
+        def weigh(r):
+            g = keep.tile([P, I], F32, name="g_%d" % r, tag="a2_%d" % (r + 1))
+            nc.scalar.activation(g[:], cc[r][:].indirect(idx5[:]), COPY)
+            nc.scalar.activation(gw[:, r, :], g[:], COPY, scale=factors[:, r : r + 1])
+
+        first_lookups(0)
+        first_lookups(1)
+        second_rows(0)
+        correct_users(0)
+        first_lookups(2)
+        correct_users(1)
+        second_rows(1)
+        first_lookups(3)
+        correct_users(2)
+        weigh(0)
+        weigh(1)
+        correct_users(3)
+        weigh(2)
+
+        last = PACK - 1
+        g_low = keep.tile([P, HALF], F32, name="g_low")
+        g_high = keep.tile([P, HALF], F32, name="g_high")
+        nc.vector.tensor_copy(g_low[:], cc[last][:].indirect(idx5[:, : LIST_COLS // 2]))
+        nc.scalar.activation(g_high[:], cc[last][:].indirect(idx5[:, LIST_COLS // 2 :]), COPY)
+        nc.vector.tensor_scalar(gw[:, last, :HALF], g_low[:], factors[:, last:], None, MULT)
+        nc.scalar.activation(gw[:, last, HALF:], g_high[:], COPY, scale=factors[:, last:])
+
+        woven = []
+        for half in range(2):
+            tile = keep.tile([P, HALF * PACK], BF16, name="woven_%d" % half, align_bytes=64)
+            nc.vector.tensor_copy(
+                tile[:].rearrange("p (c i r) -> p c r i", i=4, r=PACK),
+                gw[:, :, half * HALF : (half + 1) * HALF].rearrange("p r (c i) -> p c r i", i=4),
+            )
+            woven.append(tile)
+        for half in range(2):
+            codes = keep.tile([P, HALF], U32, name="gw_codes_%d" % half, align_bytes=64)
+            scales = keep.tile([P, HALF], U8, name="gw_scales_%d" % half, align_bytes=64)
+            nc.vector.quantize_mx(out=codes[:].bitcast(FP8X4), scales=scales[:], in_=woven[half][:])
+            for block in range(E // P):
+                bank = score_banks.tile([P, BANK], F32, name="bank")
+                nc.tensor.matmul_mx(
+                    out=bank[:, :HALF], lhsT=mix[:, 2 * block * P : 2 * (block + 1) * P].bitcast(FP4X4),
+                    lhsT_scale=mix_plane[:, block * P : (block + 1) * P],
+                    rhs=codes[:].bitcast(FP8X4), rhs_scale=scales[:], start=True, stop=True,
+                )
+                result = keep.tile([P, HALF], F32, name="result_%d_%d" % (half, block))
+                leave = nc.scalar.copy if half == 0 or block == 0 else nc.vector.tensor_copy
+                leave(result[:], bank[:, :HALF])
+                nc.sync.dma_start(out[block * P : (block + 1) * P, half * HALF : (half + 1) * HALF], result[:])

@@ -32,42 +32,50 @@ def tile_attend_correctedthen_threeq_mixed_kernel(
     nc = tc.nc
     with ExitStack() as ctx:
         keep = ctx.enter_context(tc.tile_pool(name="keep", bufs=1))
-        ring = ctx.enter_context(tc.tile_pool(name="ring", bufs=2))
-        score_banks = ctx.enter_context(tc.psum_pool(name="score_banks", bufs=6))
-        user_banks = ctx.enter_context(tc.psum_pool(name="user_banks", bufs=2))
+        shared = ctx.enter_context(tc.tile_pool(name="shared", bufs=1))
+        score_banks = ctx.enter_context(tc.psum_pool(name="score_banks", bufs=4))
+        user_banks = ctx.enter_context(tc.psum_pool(name="user_banks", bufs=4))
+
+        places = {"query": 0, "query2": 0, "picked_2": 0,
+                  "a_3": 8192, "cc_0": 8192, "a2_1": 10240, "b_3": 12288, "query2_high": 12288}
+
+        def place(name, shape, dtype, tag=""):
+            if name in places:
+                return shared.tile(shape, dtype, name=name, offset=places[name], align_bytes=64)
+            return keep.tile(shape, dtype, name=name, tag=tag or name, align_bytes=64)
 
         def load_list(name, src):
             tile = keep.tile([P, LIST_COLS], U16, name=name)
             nc.sync.dma_start(tile[:], src)
             return tile
 
-        def zeroed_plane(engine, name, width):
-            plane = keep.tile([P, width], U8, name=name, align_bytes=64)
+        def zeroed_plane(engine, name, width, tag=""):
+            plane = keep.tile([P, width], U8, name=name, tag=tag, align_bytes=64)
             engine.memset(plane[:].bitcast(I32), 0)
             return plane
 
-        def load_plane(queue, plane, src):
-            for quad in range(4):
+        def load_plane(queues, plane, src):
+            for quad, queue in enumerate(queues):
                 queue.dma_start(
                     plane[32 * quad : 32 * quad + 4, :].bitcast(I32),
                     src[0, 4 * quad : 4 * quad + 4, :].bitcast(I32),
                 )
 
-        def load_fp4(name, src):
-            words = keep.tile([P, src.shape[2]], U8, name=name, align_bytes=64)
+        def load_fp4(name, src, tag=""):
+            words = keep.tile([P, src.shape[2]], U8, name=name, tag=tag, align_bytes=64)
             nc.sync.dma_start(words[:].bitcast(I32), src[0].bitcast(I32))
             return words
 
-        def load_rows(src):
-            raw = keep.tile([P, PACK, Q], F32, name="raw")
+        def load_rows(name, src):
+            raw = place(name, [P, PACK, Q], F32)
             nc.sync.dma_start(raw[:], src.rearrange("(p j) q -> p j q", j=PACK))
             return raw
 
-        def deal(copy, name, raw, pair):
-            dealt = keep.tile([P, 2 * P * PACK], BF16, name=name, align_bytes=64)
+        def deal(copy, name, raw, first, count, tag=""):
+            dealt = place(name, [P, count * P * PACK], BF16, tag)
             copy(
-                dealt[:].rearrange("p (r m j) -> p m r j", r=2, j=PACK),
-                raw[:].rearrange("p j (m r) -> p m r j", r=PACK)[:, :, 2 * pair : 2 * pair + 2, :],
+                dealt[:].rearrange("p (r m j) -> p m r j", r=count, j=PACK),
+                raw[:].rearrange("p j (m r) -> p m r j", r=PACK)[:, :, first : first + count, :],
             )
             return dealt
 
@@ -93,46 +101,48 @@ def tile_attend_correctedthen_threeq_mixed_kernel(
         idx3 = load_list("idx3", offs3)
         idx4 = load_list("idx4", offs4)
         idx5 = load_list("idx5", offs5)
-        raw = load_rows(query)
-        load_plane(nc.scalar, keys_plane, keys_scales)
-        load_plane(nc.gpsimd, notes_plane, notes_scales)
+        factors = keep.tile([P, PACK], F32, name="factors")
+        nc.sync.dma_start(factors[:], rowf.rearrange("(p r) o -> p (r o)", r=PACK))
+        raw = load_rows("query", query)
         keys = keep.tile([P, T], U32, name="keys", align_bytes=64)
         nc.sync.dma_start(keys[:].bitcast(I32), keys_words[0].rearrange("p t j -> p (t j)").bitcast(I32))
         notes = load_fp4("notes", notes_words)
+        load_plane([nc.scalar] * 4, keys_plane, keys_scales)
+        load_plane([nc.scalar] + [nc.gpsimd] * 3, notes_plane, notes_scales)
 
-        users_plane = zeroed_plane(nc.vector, "users_plane", X)
-        mix_plane = zeroed_plane(nc.vector, "mix_plane", E)
-        f1 = [keep.tile([P, T], F32, name="f1_%d" % n) for n in range(2)]
-        f2 = keep.tile([P, X], F32, name="f2")
-        for window in f1 + [f2]:
-            nc.vector.memset(window[:], 0.0)
+        def zeroed_window(engine, name, tag=""):
+            window = place(name, [P, T], F32, tag)
+            engine.memset(window[:], 0.0)
+            return window
+
+        f1 = [zeroed_window(nc.vector, "f1_even")]
+        f2 = []
+        last = PACK - 1
+        last_factor = keep.tile([P, HALF], F32, name="last_factor")
+        nc.vector.tensor_copy(last_factor[:], factors[:, last:].to_broadcast([P, HALF]))
 
         keys_moving = [keys[:, h * BANK : (h + 1) * BANK].bitcast(FP8X4) for h in range(2)]
         notes_moving = [notes[:, 2 * h * BANK : 2 * (h + 1) * BANK].bitcast(FP4X4) for h in range(2)]
 
-        low = deal(nc.vector.tensor_copy, "query_low", raw, 0)
-        high = deal(nc.scalar.copy, "query_high", raw, 1)
+        low = deal(nc.vector.tensor_copy, "query_low", raw, 0, 2)
+        high = deal(nc.scalar.copy, "query_high", raw, 2, 2)
         rows = quantise("rows0", low[:, : P * PACK]) + quantise("rows1", low[:, P * PACK :])
         rows = rows + quantise("rows23", high[:])
 
-        raw2 = load_rows(query2)
-        users = load_fp4("users", users_words)
-        load_plane(nc.sync, users_plane, users_scales)
-        factors = keep.tile([P, PACK], F32, name="factors")
-        nc.sync.dma_start(factors[:], rowf.rearrange("(p r) o -> p (r o)", r=PACK))
-        mix = load_fp4("mix", mix_words)
-        load_plane(nc.sync, mix_plane, mix_scales)
+        raw2 = load_rows("query2", query2)
+        users = load_fp4("users", users_words, tag="query_low")
+        users_plane = zeroed_plane(nc.gpsimd, "users_plane", X, tag="query_high")
+        load_plane([nc.sync] * 4, users_plane, users_scales)
         users_moving = [users[:, 2 * h * BANK : 2 * (h + 1) * BANK].bitcast(FP4X4) for h in range(2)]
 
-        rows2 = []
         a2, cc = {}, {}
         gw = keep.tile([P, PACK, I], F32, name="gw")
 
         def first_lookups(r):
-            a = ring.tile([P, T], F32, name="a", bufs=3)
-            b = ring.tile([P, U], F32, name="b")
-            minus_a = ring.tile([P, I], F32, name="minus_a")
-            plus_b = ring.tile([P, I], F32, name="plus_b")
+            a = place("a_%d" % r, [P, T], F32)
+            b = place("b_%d" % r, [P, U], F32)
+            minus_a = place("minus_a_%d" % r, [P, I], F32)
+            plus_b = place("plus_b_%d" % r, [P, I], F32)
             helper = nc.vector.tensor_copy if r == 0 else nc.scalar.copy
             nc.scalar.copy(a[:, :BANK], scores(score_banks, rows[r], keys_moving, keys_plane, 0)[:])
             helper(a[:, BANK:], scores(score_banks, rows[r], keys_moving, keys_plane, 1)[:])
@@ -146,60 +156,81 @@ def tile_attend_correctedthen_threeq_mixed_kernel(
             else:
                 nc.scalar.activation(minus_a[:], a[:].indirect(idx[:]), COPY, scale=-1.0)
                 nc.scalar.activation(plus_b[:], b[:].indirect(idx2[:]), COPY)
-            window = f1[r % len(f1)]
+            window = f1[r % 2]
             nc.vector.tensor_tensor(window[:].indirect(idx[:]), plus_b[:], minus_a[:], ADD)
-            a2[r] = keep.tile([P, T], F32, name="a2_%d" % r, tag="a2_%d" % r)
+            a2[r] = place("a2_%d" % r, [P, T], F32)
             adder = nc.vector if r == 0 else nc.gpsimd
             adder.tensor_tensor(a2[r][:], a[:], window[:], ADD)
 
-        def second_rows(pair):
-            rows2.extend(quantise("rows2_%d" % pair, deal(nc.scalar.copy, "query2_%d" % pair, raw2, pair)[:]))
+        def move_to_users(r):
+            picked = place("picked_%d" % r, [P, I], F32)
+            nc.scalar.activation(picked[:], a2[r][:].indirect(idx3[:]), COPY)
+            nc.vector.tensor_copy(f2[min(r, 2)][:].indirect(idx4[:]), picked[:])
 
         def correct_users(r):
-            picked = ring.tile([P, I], F32, name="picked")
-            nc.scalar.activation(picked[:], a2[r][:].indirect(idx3[:]), COPY)
-            nc.vector.tensor_copy(f2[:].indirect(idx4[:]), picked[:])
-            cc[r] = ring.tile([P, X], F32, name="cc")
+            cc[r] = keep.tile([P, X], F32, name="cc_%d" % r)
             for half in range(2):
                 cols = slice(half * BANK, (half + 1) * BANK)
                 c0 = scores(user_banks, rows2[r], users_moving, users_plane, half)
-                nc.vector.tensor_tensor(cc[r][:, cols], c0[:], f2[:, cols], SUB)
+                nc.vector.tensor_tensor(cc[r][:, cols], c0[:], f2[2][:, cols], SUB)
 
-        def weigh(r):
-            g = keep.tile([P, I], F32, name="g_%d" % r, tag="a2_%d" % (r + 1))
+        def user_scores(r):
+            c0 = place("c0_%d" % r, [P, X], F32)
+            for half in range(2):
+                nc.scalar.copy(c0[:, half * BANK : (half + 1) * BANK], scores(score_banks, rows2[r], users_moving, users_plane, half)[:])
+            return c0
+
+        def correct_users_aside(r, c0, tag=""):
+            cc[r] = place("cc_%d" % r, [P, X], F32, tag)
+            nc.gpsimd.tensor_tensor(cc[r][:], c0[:], f2[r][:], SUB)
+
+        def look_up_result(r, tag):
+            g = place("g_%d" % r, [P, I], F32, tag)
             nc.scalar.activation(g[:], cc[r][:].indirect(idx5[:]), COPY)
-            nc.scalar.activation(gw[:, r, :], g[:], COPY, scale=factors[:, r : r + 1])
+            return g
 
         first_lookups(0)
+        f1.append(zeroed_window(nc.gpsimd, "f1_odd", tag="b_0"))
+        f2.append(zeroed_window(nc.gpsimd, "f2_0", tag="minus_a_0"))
+        f2.append(zeroed_window(nc.gpsimd, "f2_1", tag="a_0"))
+        f2.append(zeroed_window(nc.gpsimd, "f2_23", tag="plus_b_0"))
         first_lookups(1)
-        second_rows(0)
-        correct_users(0)
+        move_to_users(0)
+        mix = load_fp4("mix", mix_words, tag="b_1")
+        mix_plane = zeroed_plane(nc.gpsimd, "mix_plane", E, tag="minus_a_1")
+        load_plane([nc.sync] * 4, mix_plane, mix_scales)
         first_lookups(2)
-        correct_users(1)
-        second_rows(1)
+        move_to_users(1)
+        rows2 = quantise("rows2_low", deal(nc.scalar.copy, "query2_low", raw2, 0, 2, tag="b_2")[:])
         first_lookups(3)
+        rows2 = rows2 + quantise("rows2_high", deal(nc.scalar.copy, "query2_high", raw2, 2, 2)[:])
+        move_to_users(2)
         correct_users(2)
-        weigh(0)
-        weigh(1)
+        c0 = [user_scores(r) for r in range(2)]
+        correct_users_aside(0, c0[0])
+        correct_users_aside(1, c0[1], tag="b_0")
+        move_to_users(3)
         correct_users(3)
-        weigh(2)
+        for r, tag in ((2, "a2_3"), (0, "c0_0")):
+            nc.gpsimd.tensor_scalar(gw[:, r, :], look_up_result(r, tag)[:], factors[:, r : r + 1], 0.0, MULT, ADD)
+        nc.scalar.activation(gw[:, 1, :], look_up_result(1, "c0_1")[:], COPY, scale=factors[:, 1:2])
 
-        last = PACK - 1
-        g_low = keep.tile([P, HALF], F32, name="g_low")
-        g_high = keep.tile([P, HALF], F32, name="g_high")
-        nc.vector.tensor_copy(g_low[:], cc[last][:].indirect(idx5[:, : LIST_COLS // 2]))
+        g_high = place("g_high", [P, HALF], F32, "c0_1")
+        nc.vector.tensor_tensor(gw[:, last, :HALF], cc[last][:].indirect(idx5[:, : LIST_COLS // 2]), last_factor[:], MULT)
         nc.scalar.activation(g_high[:], cc[last][:].indirect(idx5[:, LIST_COLS // 2 :]), COPY)
-        nc.vector.tensor_scalar(gw[:, last, :HALF], g_low[:], factors[:, last:], None, MULT)
         nc.scalar.activation(gw[:, last, HALF:], g_high[:], COPY, scale=factors[:, last:])
 
-        woven = []
-        for half in range(2):
-            tile = keep.tile([P, HALF * PACK], BF16, name="woven_%d" % half, align_bytes=64)
-            nc.vector.tensor_copy(
-                tile[:].rearrange("p (c i r) -> p c r i", i=4, r=PACK),
-                gw[:, :, half * HALF : (half + 1) * HALF].rearrange("p r (c i) -> p c r i", i=4),
+        woven = [keep.tile([P, HALF * PACK], BF16, name="woven_%d" % half, align_bytes=64) for half in range(2)]
+
+        def weave(copy, half, first, count):
+            copy(
+                woven[half][:, first * PACK : (first + count) * PACK].rearrange("p (i r) -> p i r", r=PACK),
+                gw[:, :, half * HALF + first : half * HALF + first + count].rearrange("p r i -> p i r"),
             )
-            woven.append(tile)
+
+        weave(nc.vector.tensor_copy, 0, 0, HALF)
+        weave(nc.scalar.copy, 1, 0, HALF // 2)
+        weave(nc.vector.tensor_copy, 1, HALF // 2, HALF // 2)
         for half in range(2):
             codes = keep.tile([P, HALF], U32, name="gw_codes_%d" % half, align_bytes=64)
             scales = keep.tile([P, HALF], U8, name="gw_scales_%d" % half, align_bytes=64)

@@ -20,9 +20,28 @@ MULT = mybir.AluOpType.mult
 
 P = 128
 PACK = 4
+LAST = PACK - 1
 BANK = 512
+SIDES = T // BANK
 HALF = I // 2
 LIST_COLS = I // 16
+QUADRANT, SCALE_ROWS = 32, 4
+QUADRANTS = P // QUADRANT
+FP4_BYTES = 2
+ALIGN = 64
+ROW_BYTES = 4 * T
+
+A3_AT = PACK * Q * 4
+PLACES = {
+    "query": 0,
+    "query2": 0,
+    "picked_2": 0,
+    "a_3": A3_AT,
+    "cc_0": A3_AT,
+    "a2_1": A3_AT + ROW_BYTES // 2,
+    "b_3": A3_AT + ROW_BYTES,
+    "query2_high": A3_AT + ROW_BYTES,
+}
 
 
 def tile_attend_correctedthen_threeq_mixed_kernel(
@@ -33,36 +52,33 @@ def tile_attend_correctedthen_threeq_mixed_kernel(
     with ExitStack() as ctx:
         keep = ctx.enter_context(tc.tile_pool(name="keep", bufs=1))
         shared = ctx.enter_context(tc.tile_pool(name="shared", bufs=1))
-        score_banks = ctx.enter_context(tc.psum_pool(name="score_banks", bufs=4))
-        user_banks = ctx.enter_context(tc.psum_pool(name="user_banks", bufs=4))
+        score_banks = ctx.enter_context(tc.psum_pool(name="score_banks", bufs=2 * SIDES))
+        user_banks = ctx.enter_context(tc.psum_pool(name="user_banks", bufs=2 * SIDES))
 
-        places = {"query": 0, "query2": 0, "picked_2": 0,
-                  "a_3": 8192, "cc_0": 8192, "a2_1": 10240, "b_3": 12288, "query2_high": 12288}
-
-        def place(name, shape, dtype, tag=""):
-            if name in places:
-                return shared.tile(shape, dtype, name=name, offset=places[name], align_bytes=64)
-            return keep.tile(shape, dtype, name=name, tag=tag or name, align_bytes=64)
+        def place(name, shape, dtype, after=""):
+            if name in PLACES:
+                return shared.tile(shape, dtype, name=name, offset=PLACES[name], align_bytes=ALIGN)
+            return keep.tile(shape, dtype, name=name, tag=after or name, align_bytes=ALIGN)
 
         def load_list(name, src):
-            tile = keep.tile([P, LIST_COLS], U16, name=name)
-            nc.sync.dma_start(tile[:], src)
-            return tile
+            entries = keep.tile([P, LIST_COLS], U16, name=name)
+            nc.sync.dma_start(entries[:], src)
+            return entries
 
-        def zeroed_plane(engine, name, width, tag=""):
-            plane = keep.tile([P, width], U8, name=name, tag=tag, align_bytes=64)
+        def zeroed_plane(engine, name, width, after=""):
+            plane = keep.tile([P, width], U8, name=name, tag=after, align_bytes=ALIGN)
             engine.memset(plane[:].bitcast(I32), 0)
             return plane
 
         def load_plane(queues, plane, src):
             for quad, queue in enumerate(queues):
                 queue.dma_start(
-                    plane[32 * quad : 32 * quad + 4, :].bitcast(I32),
-                    src[0, 4 * quad : 4 * quad + 4, :].bitcast(I32),
+                    plane[QUADRANT * quad : QUADRANT * quad + SCALE_ROWS, :].bitcast(I32),
+                    src[0, SCALE_ROWS * quad : SCALE_ROWS * (quad + 1), :].bitcast(I32),
                 )
 
-        def load_fp4(name, src, tag=""):
-            words = keep.tile([P, src.shape[2]], U8, name=name, tag=tag, align_bytes=64)
+        def load_fp4(name, src, after=""):
+            words = keep.tile([P, src.shape[2]], U8, name=name, tag=after, align_bytes=ALIGN)
             nc.sync.dma_start(words[:].bitcast(I32), src[0].bitcast(I32))
             return words
 
@@ -71,178 +87,182 @@ def tile_attend_correctedthen_threeq_mixed_kernel(
             nc.sync.dma_start(raw[:], src.rearrange("(p j) q -> p j q", j=PACK))
             return raw
 
-        def deal(copy, name, raw, first, count, tag=""):
-            dealt = place(name, [P, count * P * PACK], BF16, tag)
+        def deal(copy, name, raw, first, count, after=""):
+            dealt = place(name, [P, count * P * PACK], BF16, after)
             copy(
-                dealt[:].rearrange("p (r m j) -> p m r j", r=count, j=PACK),
-                raw[:].rearrange("p j (m r) -> p m r j", r=PACK)[:, :, first : first + count, :],
+                dealt[:].rearrange("p (c m j) -> p m c j", c=count, j=PACK),
+                raw[:].rearrange("p j (m c) -> p m c j", c=PACK)[:, :, first : first + count, :],
             )
             return dealt
 
         def quantise(name, values):
             width = values.shape[1] // PACK
-            codes = keep.tile([P, width], U32, name=name + "_codes", align_bytes=64)
-            scales = keep.tile([P, width], U8, name=name + "_scales", align_bytes=64)
+            codes = keep.tile([P, width], U32, name=name + "_codes", align_bytes=ALIGN)
+            scales = keep.tile([P, width], U8, name=name + "_scales", align_bytes=ALIGN)
             nc.vector.quantize_mx(out=codes[:].bitcast(FP8X4), scales=scales[:], in_=values)
-            return [(codes[:, c : c + P].bitcast(FP8X4), scales[:, c : c + P]) for c in range(0, width, P)]
+            return [(codes[:, col : col + P].bitcast(FP8X4), scales[:, col : col + P]) for col in range(0, width, P)]
 
-        def scores(banks, rows, moving, plane, half):
+        def side_cols(side, width=1):
+            return slice(side * BANK * width, (side + 1) * BANK * width)
+
+        def scores(banks, part_rows, moving, plane, side):
             bank = banks.tile([P, BANK], F32, name="bank")
             nc.tensor.matmul_mx(
-                out=bank[:], lhsT=rows[0], lhsT_scale=rows[1], rhs=moving[half],
-                rhs_scale=plane[:, half * BANK : (half + 1) * BANK], start=True, stop=True,
+                out=bank[:], lhsT=part_rows[0], lhsT_scale=part_rows[1], rhs=moving[side],
+                rhs_scale=plane[:, side_cols(side)], start=True, stop=True,
             )
             return bank
 
-        keys_plane = zeroed_plane(nc.vector, "keys_plane", T)
-        notes_plane = zeroed_plane(nc.gpsimd, "notes_plane", U)
+        def zeroed_window(engine, name, after=""):
+            window = place(name, [P, T], F32, after)
+            engine.memset(window[:], 0.0)
+            return window
+
+        keys_plane = zeroed_plane(nc.gpsimd, "keys_plane", T)
+        notes_plane = zeroed_plane(nc.vector, "notes_plane", U)
+        raw_query = load_rows("query", query)
+        keys = keep.tile([P, T], U32, name="keys", align_bytes=ALIGN)
+        nc.sync.dma_start(keys[:].bitcast(I32), keys_words[0].rearrange("p t j -> p (t j)").bitcast(I32))
+        load_plane([nc.sync] * QUADRANTS, keys_plane, keys_scales)
+        load_plane([nc.sync] * 2 + [nc.gpsimd] * 2, notes_plane, notes_scales)
+        notes = load_fp4("notes", notes_words)
         idx = load_list("idx", offs)
         idx2 = load_list("idx2", offs2)
         idx3 = load_list("idx3", offs3)
         idx4 = load_list("idx4", offs4)
         idx5 = load_list("idx5", offs5)
         factors = keep.tile([P, PACK], F32, name="factors")
-        nc.sync.dma_start(factors[:], rowf.rearrange("(p r) o -> p (r o)", r=PACK))
-        raw = load_rows("query", query)
-        keys = keep.tile([P, T], U32, name="keys", align_bytes=64)
-        nc.sync.dma_start(keys[:].bitcast(I32), keys_words[0].rearrange("p t j -> p (t j)").bitcast(I32))
-        notes = load_fp4("notes", notes_words)
-        load_plane([nc.scalar] * 4, keys_plane, keys_scales)
-        load_plane([nc.scalar] + [nc.gpsimd] * 3, notes_plane, notes_scales)
-
-        def zeroed_window(engine, name, tag=""):
-            window = place(name, [P, T], F32, tag)
-            engine.memset(window[:], 0.0)
-            return window
+        nc.sync.dma_start(factors[:], rowf.rearrange("(p c) o -> p (c o)", c=PACK))
 
         f1 = [zeroed_window(nc.vector, "f1_even")]
         f2 = []
-        last = PACK - 1
-        last_factor = keep.tile([P, HALF], F32, name="last_factor")
-        nc.vector.tensor_copy(last_factor[:], factors[:, last:].to_broadcast([P, HALF]))
 
-        keys_moving = [keys[:, h * BANK : (h + 1) * BANK].bitcast(FP8X4) for h in range(2)]
-        notes_moving = [notes[:, 2 * h * BANK : 2 * (h + 1) * BANK].bitcast(FP4X4) for h in range(2)]
+        keys_moving = [keys[:, side_cols(side)].bitcast(FP8X4) for side in range(SIDES)]
+        notes_moving = [notes[:, side_cols(side, FP4_BYTES)].bitcast(FP4X4) for side in range(SIDES)]
 
-        low = deal(nc.vector.tensor_copy, "query_low", raw, 0, 2)
-        high = deal(nc.scalar.copy, "query_high", raw, 2, 2)
+        low = deal(nc.vector.tensor_copy, "query_low", raw_query, 0, 2)
+        high = deal(nc.scalar.copy, "query_high", raw_query, 2, 2)
         rows = quantise("rows0", low[:, : P * PACK]) + quantise("rows1", low[:, P * PACK :])
         rows = rows + quantise("rows23", high[:])
 
-        raw2 = load_rows("query2", query2)
-        users = load_fp4("users", users_words, tag="query_low")
-        users_plane = zeroed_plane(nc.gpsimd, "users_plane", X, tag="query_high")
-        load_plane([nc.sync] * 4, users_plane, users_scales)
-        users_moving = [users[:, 2 * h * BANK : 2 * (h + 1) * BANK].bitcast(FP4X4) for h in range(2)]
+        raw_query2 = load_rows("query2", query2)
+        users = load_fp4("users", users_words, after="query_low")
+        users_plane = zeroed_plane(nc.gpsimd, "users_plane", X, after="query_high")
+        load_plane([nc.sync] * QUADRANTS, users_plane, users_scales)
+        users_moving = [users[:, side_cols(side, FP4_BYTES)].bitcast(FP4X4) for side in range(SIDES)]
 
         a2, cc = {}, {}
         gw = keep.tile([P, PACK, I], F32, name="gw")
 
-        def first_lookups(r):
-            a = place("a_%d" % r, [P, T], F32)
-            b = place("b_%d" % r, [P, U], F32)
-            minus_a = place("minus_a_%d" % r, [P, I], F32)
-            plus_b = place("plus_b_%d" % r, [P, I], F32)
-            helper = nc.vector.tensor_copy if r == 0 else nc.scalar.copy
-            nc.scalar.copy(a[:, :BANK], scores(score_banks, rows[r], keys_moving, keys_plane, 0)[:])
-            helper(a[:, BANK:], scores(score_banks, rows[r], keys_moving, keys_plane, 1)[:])
-            if r == 0:
+        def replace_scores(part):
+            first = part == 0
+            a = place("a_%d" % part, [P, T], F32)
+            b = place("b_%d" % part, [P, U], F32)
+            minus_a = place("minus_a_%d" % part, [P, I], F32)
+            plus_b = place("plus_b_%d" % part, [P, I], F32)
+            empty_bank = nc.vector.tensor_copy if first else nc.scalar.copy
+            nc.scalar.copy(a[:, side_cols(0)], scores(score_banks, rows[part], keys_moving, keys_plane, 0)[:])
+            empty_bank(a[:, side_cols(1)], scores(score_banks, rows[part], keys_moving, keys_plane, 1)[:])
+            if first:
                 nc.scalar.activation(minus_a[:], a[:].indirect(idx[:]), COPY, scale=-1.0)
-            for half in range(2):
-                helper(b[:, half * BANK : (half + 1) * BANK], scores(score_banks, rows[r], notes_moving, notes_plane, half)[:])
-            if r == 0:
+            for side in range(SIDES):
+                empty_bank(b[:, side_cols(side)], scores(score_banks, rows[part], notes_moving, notes_plane, side)[:])
+            if first:
                 nc.vector.tensor_copy(plus_b[:, :HALF], b[:].indirect(idx2[:, : LIST_COLS // 2]))
                 nc.scalar.activation(plus_b[:, HALF:], b[:].indirect(idx2[:, LIST_COLS // 2 :]), COPY)
             else:
                 nc.scalar.activation(minus_a[:], a[:].indirect(idx[:]), COPY, scale=-1.0)
                 nc.scalar.activation(plus_b[:], b[:].indirect(idx2[:]), COPY)
-            window = f1[r % 2]
+            window = f1[part % 2]
             nc.vector.tensor_tensor(window[:].indirect(idx[:]), plus_b[:], minus_a[:], ADD)
-            a2[r] = place("a2_%d" % r, [P, T], F32)
-            adder = nc.vector if r == 0 else nc.gpsimd
-            adder.tensor_tensor(a2[r][:], a[:], window[:], ADD)
+            a2[part] = place("a2_%d" % part, [P, T], F32)
+            adder = nc.vector if first else nc.gpsimd
+            adder.tensor_tensor(a2[part][:], a[:], window[:], ADD)
 
-        def move_to_users(r):
-            picked = place("picked_%d" % r, [P, I], F32)
-            nc.scalar.activation(picked[:], a2[r][:].indirect(idx3[:]), COPY)
-            nc.vector.tensor_copy(f2[min(r, 2)][:].indirect(idx4[:]), picked[:])
+        def move_to_users(part):
+            picked = place("picked_%d" % part, [P, I], F32)
+            nc.scalar.activation(picked[:], a2[part][:].indirect(idx3[:]), COPY)
+            nc.vector.tensor_copy(f2[min(part, len(f2) - 1)][:].indirect(idx4[:]), picked[:])
 
-        def correct_users(r):
-            cc[r] = keep.tile([P, X], F32, name="cc_%d" % r)
-            for half in range(2):
-                cols = slice(half * BANK, (half + 1) * BANK)
-                c0 = scores(user_banks, rows2[r], users_moving, users_plane, half)
-                nc.vector.tensor_tensor(cc[r][:, cols], c0[:], f2[2][:, cols], SUB)
+        def correct_from_psum(part):
+            cc[part] = keep.tile([P, X], F32, name="cc_%d" % part)
+            for side in range(SIDES):
+                bank = scores(user_banks, rows2[part], users_moving, users_plane, side)
+                nc.vector.tensor_tensor(cc[part][:, side_cols(side)], bank[:], f2[-1][:, side_cols(side)], SUB)
 
-        def user_scores(r):
-            c0 = place("c0_%d" % r, [P, X], F32)
-            for half in range(2):
-                nc.scalar.copy(c0[:, half * BANK : (half + 1) * BANK], scores(score_banks, rows2[r], users_moving, users_plane, half)[:])
+        def user_scores(part):
+            c0 = place("c0_%d" % part, [P, X], F32)
+            for side in range(SIDES):
+                nc.scalar.copy(c0[:, side_cols(side)], scores(score_banks, rows2[part], users_moving, users_plane, side)[:])
             return c0
 
-        def correct_users_aside(r, c0, tag=""):
-            cc[r] = place("cc_%d" % r, [P, X], F32, tag)
-            nc.gpsimd.tensor_tensor(cc[r][:], c0[:], f2[r][:], SUB)
+        def correct_from_sbuf(part, c0, after=""):
+            cc[part] = place("cc_%d" % part, [P, X], F32, after)
+            nc.gpsimd.tensor_tensor(cc[part][:], c0[:], f2[part][:], SUB)
 
-        def look_up_result(r, tag):
-            g = place("g_%d" % r, [P, I], F32, tag)
-            nc.scalar.activation(g[:], cc[r][:].indirect(idx5[:]), COPY)
+        def look_up_result(part, after):
+            g = place("g_%d" % part, [P, I], F32, after)
+            nc.scalar.activation(g[:], cc[part][:].indirect(idx5[:]), COPY)
             return g
 
-        first_lookups(0)
-        f1.append(zeroed_window(nc.gpsimd, "f1_odd", tag="b_0"))
-        f2.append(zeroed_window(nc.gpsimd, "f2_0", tag="minus_a_0"))
-        f2.append(zeroed_window(nc.gpsimd, "f2_1", tag="a_0"))
-        f2.append(zeroed_window(nc.gpsimd, "f2_23", tag="plus_b_0"))
-        first_lookups(1)
+        replace_scores(0)
+        f1.append(zeroed_window(nc.gpsimd, "f1_odd", after="b_0"))
+        f2.append(zeroed_window(nc.gpsimd, "f2_0", after="minus_a_0"))
+        f2.append(zeroed_window(nc.gpsimd, "f2_1", after="a_0"))
+        f2.append(zeroed_window(nc.gpsimd, "f2_23", after="plus_b_0"))
+        replace_scores(1)
+        last_factor = place("last_factor", [P, HALF], F32, "plus_b_1")
+        nc.vector.tensor_copy(last_factor[:], factors[:, LAST:].to_broadcast([P, HALF]))
         move_to_users(0)
-        mix = load_fp4("mix", mix_words, tag="b_1")
-        mix_plane = zeroed_plane(nc.gpsimd, "mix_plane", E, tag="minus_a_1")
-        load_plane([nc.sync] * 4, mix_plane, mix_scales)
-        first_lookups(2)
+        mix = load_fp4("mix", mix_words, after="b_1")
+        mix_plane = zeroed_plane(nc.gpsimd, "mix_plane", E, after="minus_a_1")
+        load_plane([nc.sync] * QUADRANTS, mix_plane, mix_scales)
+        replace_scores(2)
         move_to_users(1)
-        rows2 = quantise("rows2_low", deal(nc.scalar.copy, "query2_low", raw2, 0, 2, tag="b_2")[:])
-        first_lookups(3)
-        rows2 = rows2 + quantise("rows2_high", deal(nc.scalar.copy, "query2_high", raw2, 2, 2)[:])
+        rows2 = quantise("rows2_low", deal(nc.scalar.copy, "query2_low", raw_query2, 0, 2, after="b_2")[:])
+        replace_scores(3)
+        rows2 = rows2 + quantise("rows2_high", deal(nc.scalar.copy, "query2_high", raw_query2, 2, 2)[:])
         move_to_users(2)
-        correct_users(2)
-        c0 = [user_scores(r) for r in range(2)]
-        correct_users_aside(0, c0[0])
-        correct_users_aside(1, c0[1], tag="b_0")
+        correct_from_psum(2)
+        c0_low = [user_scores(part) for part in range(2)]
+        correct_from_sbuf(0, c0_low[0])
+        correct_from_sbuf(1, c0_low[1], after="b_0")
         move_to_users(3)
-        correct_users(3)
-        for r, tag in ((2, "a2_3"), (0, "c0_0")):
-            nc.gpsimd.tensor_scalar(gw[:, r, :], look_up_result(r, tag)[:], factors[:, r : r + 1], 0.0, MULT, ADD)
+        correct_from_psum(3)
+
+        for part, after in ((2, "a2_3"), (0, "c0_0")):
+            nc.gpsimd.tensor_scalar(gw[:, part, :], look_up_result(part, after)[:], factors[:, part : part + 1], 0.0, MULT, ADD)
         nc.scalar.activation(gw[:, 1, :], look_up_result(1, "c0_1")[:], COPY, scale=factors[:, 1:2])
 
         g_high = place("g_high", [P, HALF], F32, "c0_1")
-        nc.vector.tensor_tensor(gw[:, last, :HALF], cc[last][:].indirect(idx5[:, : LIST_COLS // 2]), last_factor[:], MULT)
-        nc.scalar.activation(g_high[:], cc[last][:].indirect(idx5[:, LIST_COLS // 2 :]), COPY)
-        nc.scalar.activation(gw[:, last, HALF:], g_high[:], COPY, scale=factors[:, last:])
+        nc.vector.tensor_tensor(gw[:, LAST, :HALF], cc[LAST][:].indirect(idx5[:, : LIST_COLS // 2]), last_factor[:], MULT)
+        nc.scalar.activation(g_high[:], cc[LAST][:].indirect(idx5[:, LIST_COLS // 2 :]), COPY)
+        nc.scalar.activation(gw[:, LAST, HALF:], g_high[:], COPY, scale=factors[:, LAST:])
 
-        woven = [keep.tile([P, HALF * PACK], BF16, name="woven_%d" % half, align_bytes=64) for half in range(2)]
+        woven = [keep.tile([P, HALF * PACK], BF16, name="woven_%d" % half, align_bytes=ALIGN) for half in range(2)]
 
-        def weave(copy, half, first, count):
+        def weave(copy, half, start, count):
             copy(
-                woven[half][:, first * PACK : (first + count) * PACK].rearrange("p (i r) -> p i r", r=PACK),
-                gw[:, :, half * HALF + first : half * HALF + first + count].rearrange("p r i -> p i r"),
+                woven[half][:, start * PACK : (start + count) * PACK].rearrange("p (i c) -> p i c", c=PACK),
+                gw[:, :, half * HALF + start : half * HALF + start + count].rearrange("p c i -> p i c"),
             )
 
         weave(nc.vector.tensor_copy, 0, 0, HALF)
         weave(nc.scalar.copy, 1, 0, HALF // 2)
         weave(nc.vector.tensor_copy, 1, HALF // 2, HALF // 2)
         for half in range(2):
-            codes = keep.tile([P, HALF], U32, name="gw_codes_%d" % half, align_bytes=64)
-            scales = keep.tile([P, HALF], U8, name="gw_scales_%d" % half, align_bytes=64)
+            codes = keep.tile([P, HALF], U32, name="gw_codes_%d" % half, align_bytes=ALIGN)
+            scales = keep.tile([P, HALF], U8, name="gw_scales_%d" % half, align_bytes=ALIGN)
             nc.vector.quantize_mx(out=codes[:].bitcast(FP8X4), scales=scales[:], in_=woven[half][:])
             for block in range(E // P):
+                channels = slice(block * P, (block + 1) * P)
                 bank = score_banks.tile([P, BANK], F32, name="bank")
                 nc.tensor.matmul_mx(
-                    out=bank[:, :HALF], lhsT=mix[:, 2 * block * P : 2 * (block + 1) * P].bitcast(FP4X4),
-                    lhsT_scale=mix_plane[:, block * P : (block + 1) * P],
+                    out=bank[:, :HALF], lhsT=mix[:, FP4_BYTES * block * P : FP4_BYTES * (block + 1) * P].bitcast(FP4X4),
+                    lhsT_scale=mix_plane[:, channels],
                     rhs=codes[:].bitcast(FP8X4), rhs_scale=scales[:], start=True, stop=True,
                 )
                 result = keep.tile([P, HALF], F32, name="result_%d_%d" % (half, block))
-                leave = nc.scalar.copy if half == 0 or block == 0 else nc.vector.tensor_copy
-                leave(result[:], bank[:, :HALF])
-                nc.sync.dma_start(out[block * P : (block + 1) * P, half * HALF : (half + 1) * HALF], result[:])
+                last_bank = half == 1 and block == E // P - 1
+                (nc.vector.tensor_copy if last_bank else nc.scalar.copy)(result[:], bank[:, :HALF])
+                nc.sync.dma_start(out[channels, half * HALF : (half + 1) * HALF], result[:])

from contextlib import ExitStack

import concourse.mybir as mybir

D, T, U, X, I, Q, E = 512, 1024, 1024, 1024, 512, 512, 256
FLOPS = 2 * D * Q * (T + U + X) + 2 * Q * E * I

F32 = mybir.dt.float32
BF16 = mybir.dt.bfloat16
I32 = mybir.dt.int32
U32 = mybir.dt.uint32
U16 = mybir.dt.uint16
U8 = mybir.dt.uint8
FP8X4 = mybir.dt.float8_e4m3fn_x4
FP4X4 = mybir.dt.float4_e2m1fn_x4
COPY = mybir.ActivationFunctionType.Copy
ADD = mybir.AluOpType.add
SUB = mybir.AluOpType.subtract
MULT = mybir.AluOpType.mult

P = 128
PACK = 4
LAST = PACK - 1
BANK = 512
SIDES = T // BANK
HALF = I // 2
LIST_COLS = I // 16
QUADRANT, SCALE_ROWS = 32, 4
QUADRANTS = P // QUADRANT
FP4_BYTES = 2
ALIGN = 64
ROW_BYTES = 4 * T

A3_AT = PACK * Q * 4
PLACES = {
    "query": 0,
    "query2": 0,
    "picked_2": 0,
    "a_3": A3_AT,
    "cc_0": A3_AT,
    "a2_1": A3_AT + ROW_BYTES // 2,
    "b_3": A3_AT + ROW_BYTES,
    "query2_high": A3_AT + ROW_BYTES,
}


def tile_attend_correctedthen_threeq_mixed_kernel(
    tc, query, query2, keys_words, keys_scales, notes_words, notes_scales, users_words, users_scales,
    rowf, mix_words, mix_scales, offs, offs2, offs3, offs4, offs5, out,
):
    nc = tc.nc
    with ExitStack() as ctx:
        keep = ctx.enter_context(tc.tile_pool(name="keep", bufs=1))
        shared = ctx.enter_context(tc.tile_pool(name="shared", bufs=1))
        score_banks = ctx.enter_context(tc.psum_pool(name="score_banks", bufs=2 * SIDES))
        user_banks = ctx.enter_context(tc.psum_pool(name="user_banks", bufs=2 * SIDES))

        def place(name, shape, dtype, after=""):
            if name in PLACES:
                return shared.tile(shape, dtype, name=name, offset=PLACES[name], align_bytes=ALIGN)
            return keep.tile(shape, dtype, name=name, tag=after or name, align_bytes=ALIGN)

        def load_list(name, src):
            entries = keep.tile([P, LIST_COLS], U16, name=name)
            nc.sync.dma_start(entries[:], src)
            return entries

        def zeroed_plane(engine, name, width, after=""):
            plane = keep.tile([P, width], U8, name=name, tag=after, align_bytes=ALIGN)
            engine.memset(plane[:].bitcast(I32), 0)
            return plane

        def load_plane(queues, plane, src):
            for quad, queue in enumerate(queues):
                queue.dma_start(
                    plane[QUADRANT * quad : QUADRANT * quad + SCALE_ROWS, :].bitcast(I32),
                    src[0, SCALE_ROWS * quad : SCALE_ROWS * (quad + 1), :].bitcast(I32),
                )

        def load_fp4(name, src, after=""):
            words = keep.tile([P, src.shape[2]], U8, name=name, tag=after, align_bytes=ALIGN)
            nc.sync.dma_start(words[:].bitcast(I32), src[0].bitcast(I32))
            return words

        def load_rows(name, src):
            raw = place(name, [P, PACK, Q], F32)
            nc.sync.dma_start(raw[:], src.rearrange("(p j) q -> p j q", j=PACK))
            return raw

        def deal(copy, name, raw, first, count, after=""):
            dealt = place(name, [P, count * P * PACK], BF16, after)
            copy(
                dealt[:].rearrange("p (c m j) -> p m c j", c=count, j=PACK),
                raw[:].rearrange("p j (m c) -> p m c j", c=PACK)[:, :, first : first + count, :],
            )
            return dealt

        def quantise(name, values):
            width = values.shape[1] // PACK
            codes = keep.tile([P, width], U32, name=name + "_codes", align_bytes=ALIGN)
            scales = keep.tile([P, width], U8, name=name + "_scales", align_bytes=ALIGN)
            nc.vector.quantize_mx(out=codes[:].bitcast(FP8X4), scales=scales[:], in_=values)
            return [(codes[:, col : col + P].bitcast(FP8X4), scales[:, col : col + P]) for col in range(0, width, P)]

        def side_cols(side, width=1):
            return slice(side * BANK * width, (side + 1) * BANK * width)

        def scores(banks, part_rows, moving, plane, side):
            bank = banks.tile([P, BANK], F32, name="bank")
            nc.tensor.matmul_mx(
                out=bank[:], lhsT=part_rows[0], lhsT_scale=part_rows[1], rhs=moving[side],
                rhs_scale=plane[:, side_cols(side)], start=True, stop=True,
            )
            return bank

        def zeroed_window(engine, name, after=""):
            window = place(name, [P, T], F32, after)
            engine.memset(window[:], 0.0)
            return window

        keys_plane = zeroed_plane(nc.gpsimd, "keys_plane", T)
        notes_plane = zeroed_plane(nc.vector, "notes_plane", U)
        raw_query = load_rows("query", query)
        keys = keep.tile([P, T], U32, name="keys", align_bytes=ALIGN)
        nc.sync.dma_start(keys[:].bitcast(I32), keys_words[0].rearrange("p t j -> p (t j)").bitcast(I32))
        load_plane([nc.sync] * QUADRANTS, keys_plane, keys_scales)
        load_plane([nc.sync] * 2 + [nc.gpsimd] * 2, notes_plane, notes_scales)
        notes = load_fp4("notes", notes_words)
        idx = load_list("idx", offs)
        idx2 = load_list("idx2", offs2)
        idx3 = load_list("idx3", offs3)
        idx4 = load_list("idx4", offs4)
        idx5 = load_list("idx5", offs5)
        factors = keep.tile([P, PACK], F32, name="factors")
        nc.sync.dma_start(factors[:], rowf.rearrange("(p c) o -> p (c o)", c=PACK))

        f1 = [zeroed_window(nc.vector, "f1_even")]
        f2 = []

        keys_moving = [keys[:, side_cols(side)].bitcast(FP8X4) for side in range(SIDES)]
        notes_moving = [notes[:, side_cols(side, FP4_BYTES)].bitcast(FP4X4) for side in range(SIDES)]

        low = deal(nc.vector.tensor_copy, "query_low", raw_query, 0, 2)
        high = deal(nc.scalar.copy, "query_high", raw_query, 2, 2)
        rows = quantise("rows0", low[:, : P * PACK]) + quantise("rows1", low[:, P * PACK :])
        rows = rows + quantise("rows23", high[:])

        raw_query2 = load_rows("query2", query2)
        users = load_fp4("users", users_words, after="query_low")
        users_plane = zeroed_plane(nc.gpsimd, "users_plane", X, after="query_high")
        load_plane([nc.sync] * QUADRANTS, users_plane, users_scales)
        users_moving = [users[:, side_cols(side, FP4_BYTES)].bitcast(FP4X4) for side in range(SIDES)]

        a2, cc = {}, {}
        gw = keep.tile([P, PACK, I], F32, name="gw")

        def replace_scores(part):
            first = part == 0
            a = place("a_%d" % part, [P, T], F32)
            b = place("b_%d" % part, [P, U], F32)
            minus_a = place("minus_a_%d" % part, [P, I], F32)
            plus_b = place("plus_b_%d" % part, [P, I], F32)
            empty_bank = nc.vector.tensor_copy if first else nc.scalar.copy
            nc.scalar.copy(a[:, side_cols(0)], scores(score_banks, rows[part], keys_moving, keys_plane, 0)[:])
            empty_bank(a[:, side_cols(1)], scores(score_banks, rows[part], keys_moving, keys_plane, 1)[:])
            if first:
                nc.scalar.activation(minus_a[:], a[:].indirect(idx[:]), COPY, scale=-1.0)
            for side in range(SIDES):
                empty_bank(b[:, side_cols(side)], scores(score_banks, rows[part], notes_moving, notes_plane, side)[:])
            if first:
                nc.vector.tensor_copy(plus_b[:, :HALF], b[:].indirect(idx2[:, : LIST_COLS // 2]))
                nc.scalar.activation(plus_b[:, HALF:], b[:].indirect(idx2[:, LIST_COLS // 2 :]), COPY)
            else:
                nc.scalar.activation(minus_a[:], a[:].indirect(idx[:]), COPY, scale=-1.0)
                nc.scalar.activation(plus_b[:], b[:].indirect(idx2[:]), COPY)
            window = f1[part % 2]
            nc.vector.tensor_tensor(window[:].indirect(idx[:]), plus_b[:], minus_a[:], ADD)
            a2[part] = place("a2_%d" % part, [P, T], F32)
            adder = nc.vector if first else nc.gpsimd
            adder.tensor_tensor(a2[part][:], a[:], window[:], ADD)

        def move_to_users(part):
            picked = place("picked_%d" % part, [P, I], F32)
            nc.scalar.activation(picked[:], a2[part][:].indirect(idx3[:]), COPY)
            nc.vector.tensor_copy(f2[min(part, len(f2) - 1)][:].indirect(idx4[:]), picked[:])

        def correct_from_psum(part):
            cc[part] = keep.tile([P, X], F32, name="cc_%d" % part)
            for side in range(SIDES):
                bank = scores(user_banks, rows2[part], users_moving, users_plane, side)
                nc.vector.tensor_tensor(cc[part][:, side_cols(side)], bank[:], f2[-1][:, side_cols(side)], SUB)

        def user_scores(part):
            c0 = place("c0_%d" % part, [P, X], F32)
            for side in range(SIDES):
                nc.scalar.copy(c0[:, side_cols(side)], scores(score_banks, rows2[part], users_moving, users_plane, side)[:])
            return c0

        def correct_from_sbuf(part, c0, after=""):
            cc[part] = place("cc_%d" % part, [P, X], F32, after)
            nc.gpsimd.tensor_tensor(cc[part][:], c0[:], f2[part][:], SUB)

        def look_up_result(part, after):
            g = place("g_%d" % part, [P, I], F32, after)
            nc.scalar.activation(g[:], cc[part][:].indirect(idx5[:]), COPY)
            return g

        replace_scores(0)
        f1.append(zeroed_window(nc.gpsimd, "f1_odd", after="b_0"))
        f2.append(zeroed_window(nc.gpsimd, "f2_0", after="minus_a_0"))
        f2.append(zeroed_window(nc.gpsimd, "f2_1", after="a_0"))
        f2.append(zeroed_window(nc.gpsimd, "f2_23", after="plus_b_0"))
        replace_scores(1)
        last_factor = place("last_factor", [P, HALF], F32, "plus_b_1")
        nc.vector.tensor_copy(last_factor[:], factors[:, LAST:].to_broadcast([P, HALF]))
        move_to_users(0)
        mix = load_fp4("mix", mix_words, after="b_1")
        mix_plane = zeroed_plane(nc.gpsimd, "mix_plane", E, after="minus_a_1")
        load_plane([nc.sync] * QUADRANTS, mix_plane, mix_scales)
        replace_scores(2)
        move_to_users(1)
        rows2 = quantise("rows2_low", deal(nc.scalar.copy, "query2_low", raw_query2, 0, 2, after="b_2")[:])
        replace_scores(3)
        rows2 = rows2 + quantise("rows2_high", deal(nc.scalar.copy, "query2_high", raw_query2, 2, 2)[:])
        move_to_users(2)
        correct_from_psum(2)
        c0_low = [user_scores(part) for part in range(2)]
        correct_from_sbuf(0, c0_low[0])
        correct_from_sbuf(1, c0_low[1], after="b_0")
        move_to_users(3)
        correct_from_psum(3)

        for part, after in ((2, "a2_3"), (0, "c0_0")):
            nc.gpsimd.tensor_scalar(gw[:, part, :], look_up_result(part, after)[:], factors[:, part : part + 1], 0.0, MULT, ADD)
        nc.scalar.activation(gw[:, 1, :], look_up_result(1, "c0_1")[:], COPY, scale=factors[:, 1:2])

        g_high = place("g_high", [P, HALF], F32, "c0_1")
        nc.vector.tensor_tensor(gw[:, LAST, :HALF], cc[LAST][:].indirect(idx5[:, : LIST_COLS // 2]), last_factor[:], MULT)
        nc.scalar.activation(g_high[:], cc[LAST][:].indirect(idx5[:, LIST_COLS // 2 :]), COPY)
        nc.scalar.activation(gw[:, LAST, HALF:], g_high[:], COPY, scale=factors[:, LAST:])

        woven = [keep.tile([P, HALF * PACK], BF16, name="woven_%d" % half, align_bytes=ALIGN) for half in range(2)]

        def weave(copy, half, start, count):
            copy(
                woven[half][:, start * PACK : (start + count) * PACK].rearrange("p (i c) -> p i c", c=PACK),
                gw[:, :, half * HALF + start : half * HALF + start + count].rearrange("p c i -> p i c"),
            )

        weave(nc.vector.tensor_copy, 0, 0, HALF)
        weave(nc.scalar.copy, 1, 0, HALF // 2)
        weave(nc.vector.tensor_copy, 1, HALF // 2, HALF // 2)
        for half in range(2):
            codes = keep.tile([P, HALF], U32, name="gw_codes_%d" % half, align_bytes=ALIGN)
            scales = keep.tile([P, HALF], U8, name="gw_scales_%d" % half, align_bytes=ALIGN)
            nc.vector.quantize_mx(out=codes[:].bitcast(FP8X4), scales=scales[:], in_=woven[half][:])
            for block in range(E // P):
                channels = slice(block * P, (block + 1) * P)
                bank = score_banks.tile([P, BANK], F32, name="bank")
                nc.tensor.matmul_mx(
                    out=bank[:, :HALF], lhsT=mix[:, FP4_BYTES * block * P : FP4_BYTES * (block + 1) * P].bitcast(FP4X4),
                    lhsT_scale=mix_plane[:, channels],
                    rhs=codes[:].bitcast(FP8X4), rhs_scale=scales[:], start=True, stop=True,
                )
                result = keep.tile([P, HALF], F32, name="result_%d_%d" % (half, block))
                last_bank = half == 1 and block == E // P - 1
                (nc.vector.tensor_copy if last_bank else nc.scalar.copy)(result[:], bank[:, :HALF])
                nc.sync.dma_start(out[channels, half * HALF : (half + 1) * HALF], result[:])
